import numpy as np
import ml_dtypes


def mxq(x, axis, fmt="e4m3"):
    dtype, down = {"e4m3": (ml_dtypes.float8_e4m3fn, 7), "e5m2": (ml_dtypes.float8_e5m2, 14)}[fmt]
    v = np.moveaxis(np.asarray(x, np.float32).astype(ml_dtypes.bfloat16).astype(np.float64), axis, -1)
    blocks = v.reshape(v.shape[:-1] + (-1, 32))
    amax = np.abs(blocks).max(-1, keepdims=True)
    byte = np.maximum(np.where(amax > 0, np.frexp(amax)[1] - 1 + 127, 0) - down, 1)
    scale = np.exp2(byte - 127.0)
    codes = (blocks / scale).astype(np.float32).astype(dtype).astype(np.float64)
    return np.moveaxis((codes * scale).reshape(v.shape), -1, axis)


WIDE = False


def mx_kscale(k):
    if not WIDE:
        return np.ones(k)
    levels = np.array([10, -10, 5, -5, 0])
    if k % 512:
        return np.exp2(np.random.permutation(np.resize(levels, k // 32))).repeat(32)
    a = np.empty((k // 512, 16))
    for p in range(k // 512):
        a[p, :8] = np.random.permutation(np.resize(levels, 8))
        for g in range(8):
            far = levels[np.abs(levels - a[p, g]) >= 10]
            a[p, g + 8] = far[np.random.randint(len(far))]
    return np.exp2(a.ravel()).repeat(32)


def f64(x):
    return np.asarray(x).astype(np.float64)


def striped(idx):
    return np.tile(np.asarray(idx).reshape(-1, 16).T, (8, 1)).astype(np.uint16)


def unstriped(offs):
    return offs[:16].T.reshape(-1).astype(np.int64)


E2M1 = np.array([0.0, 0.5, 1.0, 1.5, 2.0, 3.0, 4.0, 6.0, -0.0, -0.5, -1.0, -1.5, -2.0, -3.0, -4.0, -6.0])


def pack_weight(w, fmt):
    k, n = w.shape
    w = f64(np.asarray(w, np.float32).astype(ml_dtypes.bfloat16)).reshape(k // 32, 32, n)
    amax = np.abs(w).max(1)
    if fmt == "e4m3":
        byte = np.frexp(amax)[1] - 1 + 127 - 7
    else:
        mant, ex = np.frexp(amax / 6.0)
        byte = np.where(mant > 0.5, ex, ex - 1) + 127
    byte = np.clip(np.where(amax > 0, byte, 1), 1, 254)
    scaled = (w * np.exp2(127.0 - byte)[:, None, :]).reshape(k, n).astype(np.float32)
    by_word = np.ascontiguousarray(scaled.reshape(k // 512, 128, 4, n).transpose(0, 1, 3, 2))
    if fmt == "e4m3":
        words = by_word.astype(ml_dtypes.float8_e4m3fn).view(np.uint8)
    else:
        c = by_word.astype(ml_dtypes.float4_e2m1fn).view(np.uint8) & 0xF
        words = (c[..., 0::2] | (c[..., 1::2] << 4)).reshape(k // 512, 128, 2 * n)
    return np.ascontiguousarray(words), np.ascontiguousarray(byte.astype(np.uint8).reshape(k // 512, 16, n))


def unpack_weight(words, scales, fmt):
    g, _, n = scales.shape
    words = np.ascontiguousarray(words).reshape(g, 128, n, -1)
    if fmt == "e4m3":
        vals = words.view(ml_dtypes.float8_e4m3fn).astype(np.float64)
    else:
        nib = np.empty((g, 128, n, 4), np.uint8)
        nib[..., 0::2] = words & 0xF
        nib[..., 1::2] = words >> 4
        vals = E2M1[nib]
    vals = vals * np.repeat(np.exp2(scales.astype(np.float64) - 127.0), 8, axis=1)[..., None]
    return vals.transpose(0, 1, 3, 2).reshape(g * 512, n)


def bf(x):
    return np.asarray(x, np.float32).astype(ml_dtypes.bfloat16)


def planes(Y):
    r, m = Y.shape
    b = f64(bf(Y)).reshape(r // 32, 32, m)
    amax = np.abs(b).max(1)
    byte = np.clip(np.where(amax > 0, np.frexp(amax)[1] - 1 + 127 - 7, 1), 1, 254)
    codes = (b * np.exp2(127.0 - byte)[:, None, :]).reshape(r, m).astype(np.float32).astype(ml_dtypes.float8_e4m3fn).view(np.uint8)
    words = codes.reshape(r // 512, 128, 4, m).transpose(0, 1, 3, 2)
    return np.ascontiguousarray(words), np.ascontiguousarray(byte.astype(np.uint8).reshape(r // 512, 16, m))


D, T, I, C, E = 512, 2048, 512, 512, 512


def setup_inputs():
    n = np.random.standard_normal
    idx = np.random.permutation(T)[:I]
    fd = mx_kscale(D)
    fc = mx_kscale(C)
    keysp = pack_weight(n((D, T)) / fd[:, None], "e4m3")
    return {
        "keys_words": keysp[0],
        "keys_scales": keysp[1],
        "kcopy": (n((E, T))).astype(np.float32),
        "wd": (n((D, C)) * 1 / np.sqrt(D) * fd[:, None] * fc).astype(np.float32),
        "wu": (n((C, E)) * 0.7 / np.sqrt(C) / fc[:, None]).astype(np.float32),
        "offs": striped(idx),
    }


def reference(keys_words, keys_scales, kcopy, wd, wu, offs):
    idx = unstriped(offs)
    keysu = unpack_weight(keys_words, keys_scales, "e4m3")
    wdq = mxq(f64(wd), 0, "e4m3")
    keysidxg = keysu[:, idx]
    z = wdq.T @ keysidxg
    wuq = mxq(f64(wu), 0, "e4m3")
    zq = mxq(z, 0, "e4m3")
    v = wuq.T @ zq
    y = f64(kcopy)[:, idx] + v
    words, scales = planes(y)
    return y, words, scales

@@ -1,0 +1,171 @@
+from contextlib import ExitStack
+
+import concourse.mybir as mybir
+
+D, T, I, C, E = 512, 2048, 512, 512, 512
+FLOPS = 2 * D * C * I + 2 * C * E * I
+
+F32 = mybir.dt.float32
+BF16 = mybir.dt.bfloat16
+I32 = mybir.dt.int32
+U32 = mybir.dt.uint32
+U16 = mybir.dt.uint16
+U8 = mybir.dt.uint8
+FP8X4 = mybir.dt.float8_e4m3fn_x4
+ADD = mybir.AluOpType.add
+
+P = 128
+PACK = 4
+Z_SLOTS = 128
+TAIL_SLOTS = 128
+WD_SCALAR_COLS = 48
+
+
+def deal_weights(copy, raw, grouped, m0, m1):
+    copy(
+        out=grouped[:].rearrange("p (t m j) -> p m t j", t=PACK, j=PACK)[:, m0:m1],
+        in_=raw[:].rearrange("p j (m t) -> p m t j", t=PACK)[:, m0:m1],
+    )
+
+
+def tile_attend_latenterror_pl_kernel(tc, keys_words, keys_scales, kcopy, wd, wu, offs, out_0, out_1, out_2):
+    nc = tc.nc
+    with ExitStack() as ctx:
+        sb = ctx.enter_context(tc.tile_pool(name="sb", bufs=1))
+        psum = ctx.enter_context(tc.psum_pool(name="psum", bufs=1))
+
+        offsets = sb.tile([P, I // 16], U16, name="offsets")
+        nc.sync.dma_start(offsets[:], offs)
+
+        pool_scales = sb.tile([P, T], U8, name="pool_scales")
+        nc.vector.memset(pool_scales[:].bitcast(I32), 0)
+
+        wd_raw = sb.tile([P, PACK, C], F32, name="wd_raw")
+        nc.sync.dma_start(out=wd_raw[:], in_=wd.rearrange("(p j) c -> p j c", j=PACK))
+        for q in range(4):
+            nc.scalar.dma_start(
+                out=pool_scales[32 * q : 32 * q + 4, :].bitcast(I32),
+                in_=keys_scales[0, 4 * q : 4 * q + 4, :].bitcast(I32),
+            )
+        pool_words = sb.tile([P, T], U32, name="pool_words")
+        nc.sync.dma_start(
+            out=pool_words[:].bitcast(I32),
+            in_=keys_words[0].rearrange("p n t -> p (n t)").bitcast(I32),
+        )
+        wu_raw = sb.tile([P, PACK, E], F32, name="wu_raw")
+        nc.sync.dma_start(out=wu_raw[:], in_=wu.rearrange("(p j) e -> p j e", j=PACK))
+        kcopy_rows = kcopy.rearrange("(p t) n -> p t n", t=PACK)
+        kc = []
+        for t in range(PACK):
+            plane = sb.tile([P, T], F32, name=f"kc{t}")
+            nc.sync.dma_start(out=plane[:], in_=kcopy_rows[:, t, :])
+            kc.append(plane)
+
+        key_scales = sb.tile([P, I], U8, name="key_scales", align_bytes=64)
+        nc.vector.tensor_copy(out=key_scales[:], in_=pool_scales[:].indirect(offsets[:]))
+
+        wd_bf = sb.tile([P, C * PACK], BF16, name="wd_bf", align_bytes=64)
+        deal_weights(nc.scalar.copy, wd_raw, wd_bf, 0, WD_SCALAR_COLS)
+        deal_weights(nc.vector.tensor_copy, wd_raw, wd_bf, WD_SCALAR_COLS, P)
+        wd_codes = sb.tile([P, C], U32, name="wd_codes", align_bytes=64)
+        wd_scales = sb.tile([P, C], U8, name="wd_scales", align_bytes=64)
+        nc.vector.quantize_mx(out=wd_codes[:].bitcast(FP8X4), scales=wd_scales[:], in_=wd_bf[:])
+
+        key_words = sb.tile([P, I], U32, name="key_words", align_bytes=64)
+        for h in range(2):
+            nc.vector.tensor_copy(
+                out=key_words[:, 256 * h : 256 * (h + 1)],
+                in_=pool_words[:].indirect(offsets[:, 16 * h : 16 * (h + 1)]),
+            )
+
+        wu_bf = sb.tile([P, E * PACK], BF16, name="wu_bf", align_bytes=64)
+        deal_weights(nc.vector.tensor_copy, wu_raw, wu_bf, 0, P)
+        wu_codes = sb.tile([P, E], U32, name="wu_codes", align_bytes=64)
+        wu_scales = sb.tile([P, E], U8, name="wu_scales", align_bytes=64)
+        nc.vector.quantize_mx(out=wu_codes[:].bitcast(FP8X4), scales=wu_scales[:], in_=wu_bf[:])
+
+        z_bf = sb.tile([P, I * PACK], BF16, name="z_bf", align_bytes=64)
+        z_codes = sb.tile([P, I], U32, name="z_codes", align_bytes=64)
+        z_scales = sb.tile([P, I], U8, name="z_scales", align_bytes=64)
+        for s in range(I // Z_SLOTS):
+            slots = slice(s * Z_SLOTS, (s + 1) * Z_SLOTS)
+            bank = psum.tile([P, PACK, Z_SLOTS], F32, name=f"z_bank{s}")
+            for t in range(PACK):
+                cols = slice(t * P, (t + 1) * P)
+                nc.tensor.matmul_mx(
+                    out=bank[:, t, :],
+                    lhsT=wd_codes[:, cols].bitcast(FP8X4),
+                    lhsT_scale=wd_scales[:, cols],
+                    rhs=key_words[:, slots].bitcast(FP8X4),
+                    rhs_scale=key_scales[:, slots],
+                    start=True,
+                    stop=True,
+                )
+            nc.scalar.copy(
+                out=z_bf[:, s * Z_SLOTS * PACK : (s + 1) * Z_SLOTS * PACK].rearrange("p (n t) -> p n t", t=PACK),
+                in_=bank[:].rearrange("p t n -> p n t"),
+            )
+            if s % 2 == 1:
+                half = slice((s - 1) * Z_SLOTS, (s + 1) * Z_SLOTS)
+                nc.vector.quantize_mx(
+                    out=z_codes[:, half].bitcast(FP8X4),
+                    scales=z_scales[:, half],
+                    in_=z_bf[:, half.start * PACK : half.stop * PACK],
+                )
+
+        v = []
+        for t in range(PACK):
+            cols = slice(t * P, (t + 1) * P)
+            bank = psum.tile([P, I], F32, name=f"v_bank{t}")
+            nc.tensor.matmul_mx(
+                out=bank[:],
+                lhsT=wu_codes[:, cols].bitcast(FP8X4),
+                lhsT_scale=wu_scales[:, cols],
+                rhs=z_codes[:].bitcast(FP8X4),
+                rhs_scale=z_scales[:],
+                start=True,
+                stop=True,
+            )
+            v_t = sb.tile([P, I], F32, name=f"v{t}")
+            nc.scalar.copy(out=v_t[:], in_=bank[:])
+            v.append(v_t)
+
+        out_rows = out_0.rearrange("(p t) i -> p t i", t=PACK)
+        y = [sb.tile([P, 2, I], F32, name=f"y{u}") for u in range(2)]
+        y_bf = sb.tile([P, I, PACK], BF16, name="y_bf", align_bytes=64)
+        y_codes = sb.tile([P, I], U32, name="y_codes", align_bytes=64)
+        y_scales = sb.tile([P, I], U8, name="y_scales", align_bytes=64)
+        for t in range(3):
+            nc.vector.tensor_tensor(y[t // 2][:, t % 2, :], kc[t][:].indirect(offsets[:]), v[t][:], ADD)
+            if t == 1:
+                nc.sync.dma_start(out=out_rows[:, 0:2, :], in_=y[0][:])
+                nc.scalar.copy(out=y_bf[:, :, 0:2], in_=y[0][:].rearrange("p t i -> p i t"))
+        nc.sync.dma_start(out=out_rows[:, 2, :], in_=y[1][:, 0, :])
+        words_out = out_1[0].rearrange("p i t -> p (i t)").bitcast(I32)
+        n_tail = I // TAIL_SLOTS
+        for s in range(n_tail):
+            slots = slice(s * TAIL_SLOTS, (s + 1) * TAIL_SLOTS)
+            nc.vector.tensor_tensor(
+                y[1][:, 1, slots],
+                kc[3][:].indirect(offsets[:, slots.start // 16 : slots.stop // 16]),
+                v[3][:, slots],
+                ADD,
+            )
+            nc.scalar.copy(out=y_bf[:, slots, 2:4], in_=y[1][:, :, slots].rearrange("p t i -> p i t"))
+            if s % 2 == 1:
+                half = slice((s - 1) * TAIL_SLOTS, (s + 1) * TAIL_SLOTS)
+                nc.sync.dma_start(out=out_rows[:, 3, half], in_=y[1][:, 1, half])
+        for h in range(2):
+            half = slice(256 * h, 256 * (h + 1))
+            nc.vector.quantize_mx(
+                out=y_codes[:, half].bitcast(FP8X4),
+                scales=y_scales[:, half],
+                in_=y_bf[:, half, :].rearrange("p i t -> p (i t)"),
+            )
+            nc.sync.dma_start(out=words_out[:, half], in_=y_codes[:, half].bitcast(I32))
+        for q in range(4):
+            eng = nc.scalar if q % 2 == 0 else nc.sync
+            eng.dma_start(
+                out=out_2[0, 4 * q : 4 * q + 4, :].bitcast(I32),
+                in_=y_scales[32 * q : 32 * q + 4, :].bitcast(I32),
+            )

@@ -23,8 +23,8 @@ WD_SCALAR_COLS = 48
 
 def deal_weights(copy, raw, grouped, m0, m1):
     copy(
-        out=grouped[:].rearrange("p (t m j) -> p m t j", t=PACK, j=PACK)[:, m0:m1],
-        in_=raw[:].rearrange("p j (m t) -> p m t j", t=PACK)[:, m0:m1],
+        out=grouped[:].rearrange("p (t m j) -> p m j t", t=PACK, j=PACK)[:, m0:m1],
+        in_=raw[:].rearrange("p j (m t) -> p m j t", t=PACK)[:, m0:m1],
     )
 
 
@@ -43,15 +43,15 @@ def tile_attend_latenterror_pl_kernel(tc, keys_words, keys_scales, kcopy, wd, wu
         wd_raw = sb.tile([P, PACK, C], F32, name="wd_raw")
         nc.sync.dma_start(out=wd_raw[:], in_=wd.rearrange("(p j) c -> p j c", j=PACK))
         for q in range(4):
-            nc.scalar.dma_start(
+            nc.sync.dma_start(
                 out=pool_scales[32 * q : 32 * q + 4, :].bitcast(I32),
                 in_=keys_scales[0, 4 * q : 4 * q + 4, :].bitcast(I32),
             )
         pool_words = sb.tile([P, T], U32, name="pool_words")
-        nc.sync.dma_start(
-            out=pool_words[:].bitcast(I32),
-            in_=keys_words[0].rearrange("p n t -> p (n t)").bitcast(I32),
-        )
+        words_in = keys_words[0].rearrange("p n t -> p (n t)").bitcast(I32)
+        for h in range(2):
+            cols = slice(h * T // 2, (h + 1) * T // 2)
+            nc.sync.dma_start(out=pool_words[:, cols].bitcast(I32), in_=words_in[:, cols])
         wu_raw = sb.tile([P, PACK, E], F32, name="wu_raw")
         nc.sync.dma_start(out=wu_raw[:], in_=wu.rearrange("(p j) e -> p j e", j=PACK))
         kcopy_rows = kcopy.rearrange("(p t) n -> p t n", t=PACK)
@@ -61,15 +61,15 @@ def tile_attend_latenterror_pl_kernel(tc, keys_words, keys_scales, kcopy, wd, wu
             nc.sync.dma_start(out=plane[:], in_=kcopy_rows[:, t, :])
             kc.append(plane)
 
-        key_scales = sb.tile([P, I], U8, name="key_scales", align_bytes=64)
-        nc.vector.tensor_copy(out=key_scales[:], in_=pool_scales[:].indirect(offsets[:]))
-
-        wd_bf = sb.tile([P, C * PACK], BF16, name="wd_bf", align_bytes=64)
+        wd_bf = sb.tile([P, C * PACK], BF16, name="wd_bf", tag="w_bf", align_bytes=64)
         deal_weights(nc.scalar.copy, wd_raw, wd_bf, 0, WD_SCALAR_COLS)
         deal_weights(nc.vector.tensor_copy, wd_raw, wd_bf, WD_SCALAR_COLS, P)
         wd_codes = sb.tile([P, C], U32, name="wd_codes", align_bytes=64)
         wd_scales = sb.tile([P, C], U8, name="wd_scales", align_bytes=64)
         nc.vector.quantize_mx(out=wd_codes[:].bitcast(FP8X4), scales=wd_scales[:], in_=wd_bf[:])
+
+        key_scales = sb.tile([P, I], U8, name="key_scales", align_bytes=64)
+        nc.vector.tensor_copy(out=key_scales[:], in_=pool_scales[:].indirect(offsets[:]))
 
         key_words = sb.tile([P, I], U32, name="key_words", align_bytes=64)
         for h in range(2):
@@ -78,14 +78,14 @@ def tile_attend_latenterror_pl_kernel(tc, keys_words, keys_scales, kcopy, wd, wu
                 in_=pool_words[:].indirect(offsets[:, 16 * h : 16 * (h + 1)]),
             )
 
-        wu_bf = sb.tile([P, E * PACK], BF16, name="wu_bf", align_bytes=64)
+        wu_bf = sb.tile([P, E * PACK], BF16, name="wu_bf", tag="w_bf", align_bytes=64)
         deal_weights(nc.vector.tensor_copy, wu_raw, wu_bf, 0, P)
         wu_codes = sb.tile([P, E], U32, name="wu_codes", align_bytes=64)
         wu_scales = sb.tile([P, E], U8, name="wu_scales", align_bytes=64)
         nc.vector.quantize_mx(out=wu_codes[:].bitcast(FP8X4), scales=wu_scales[:], in_=wu_bf[:])
 
         z_bf = sb.tile([P, I * PACK], BF16, name="z_bf", align_bytes=64)
-        z_codes = sb.tile([P, I], U32, name="z_codes", align_bytes=64)
+        z_codes = sb.tile([P, I], U32, name="z_codes", tag="w_bf", align_bytes=64)
         z_scales = sb.tile([P, I], U8, name="z_scales", align_bytes=64)
         for s in range(I // Z_SLOTS):
             slots = slice(s * Z_SLOTS, (s + 1) * Z_SLOTS)

@@ -18,7 +18,7 @@ P = 128
 PACK = 4
 Z_SLOTS = 128
 TAIL_SLOTS = 128
-WD_SCALAR_COLS = 48
+WD_SCALAR_COLS = 76
 
 
 def deal_weights(copy, raw, grouped, m0, m1):
@@ -35,7 +35,6 @@ def tile_attend_latenterror_pl_kernel(tc, keys_words, keys_scales, kcopy, wd, wu
         psum = ctx.enter_context(tc.psum_pool(name="psum", bufs=1))
 
         offsets = sb.tile([P, I // 16], U16, name="offsets")
-        nc.sync.dma_start(offsets[:], offs)
 
         pool_scales = sb.tile([P, T], U8, name="pool_scales")
         nc.vector.memset(pool_scales[:].bitcast(I32), 0)
@@ -47,12 +46,12 @@ def tile_attend_latenterror_pl_kernel(tc, keys_words, keys_scales, kcopy, wd, wu
                 out=pool_scales[32 * q : 32 * q + 4, :].bitcast(I32),
                 in_=keys_scales[0, 4 * q : 4 * q + 4, :].bitcast(I32),
             )
+        nc.sync.dma_start(offsets[:], offs)
         pool_words = sb.tile([P, T], U32, name="pool_words")
-        words_in = keys_words[0].rearrange("p n t -> p (n t)").bitcast(I32)
-        for h in range(2):
-            cols = slice(h * T // 2, (h + 1) * T // 2)
-            nc.sync.dma_start(out=pool_words[:, cols].bitcast(I32), in_=words_in[:, cols])
-        wu_raw = sb.tile([P, PACK, E], F32, name="wu_raw")
+        nc.sync.dma_start(
+            out=pool_words[:].bitcast(I32), in_=keys_words[0].rearrange("p n t -> p (n t)").bitcast(I32)
+        )
+        wu_raw = sb.tile([P, PACK, E], F32, name="wu_raw", tag="wu_raw", align_bytes=64)
         nc.sync.dma_start(out=wu_raw[:], in_=wu.rearrange("(p j) e -> p j e", j=PACK))
         kcopy_rows = kcopy.rearrange("(p t) n -> p t n", t=PACK)
         kc = []
@@ -64,12 +63,11 @@ def tile_attend_latenterror_pl_kernel(tc, keys_words, keys_scales, kcopy, wd, wu
         wd_bf = sb.tile([P, C * PACK], BF16, name="wd_bf", tag="w_bf", align_bytes=64)
         deal_weights(nc.scalar.copy, wd_raw, wd_bf, 0, WD_SCALAR_COLS)
         deal_weights(nc.vector.tensor_copy, wd_raw, wd_bf, WD_SCALAR_COLS, P)
+        key_scales = sb.tile([P, I], U8, name="key_scales", align_bytes=64)
+        nc.vector.tensor_copy(out=key_scales[:], in_=pool_scales[:].indirect(offsets[:]))
         wd_codes = sb.tile([P, C], U32, name="wd_codes", align_bytes=64)
         wd_scales = sb.tile([P, C], U8, name="wd_scales", align_bytes=64)
         nc.vector.quantize_mx(out=wd_codes[:].bitcast(FP8X4), scales=wd_scales[:], in_=wd_bf[:])
-
-        key_scales = sb.tile([P, I], U8, name="key_scales", align_bytes=64)
-        nc.vector.tensor_copy(out=key_scales[:], in_=pool_scales[:].indirect(offsets[:]))
 
         key_words = sb.tile([P, I], U32, name="key_words", align_bytes=64)
         for h in range(2):
@@ -82,10 +80,9 @@ def tile_attend_latenterror_pl_kernel(tc, keys_words, keys_scales, kcopy, wd, wu
         deal_weights(nc.vector.tensor_copy, wu_raw, wu_bf, 0, P)
         wu_codes = sb.tile([P, E], U32, name="wu_codes", align_bytes=64)
         wu_scales = sb.tile([P, E], U8, name="wu_scales", align_bytes=64)
-        nc.vector.quantize_mx(out=wu_codes[:].bitcast(FP8X4), scales=wu_scales[:], in_=wu_bf[:])
 
-        z_bf = sb.tile([P, I * PACK], BF16, name="z_bf", align_bytes=64)
-        z_codes = sb.tile([P, I], U32, name="z_codes", tag="w_bf", align_bytes=64)
+        z_bf = sb.tile([P, I * PACK], BF16, name="z_bf", tag="z_bf", align_bytes=64)
+        z_codes = sb.tile([P, I], U32, name="z_codes", tag="wu_raw", align_bytes=64)
         z_scales = sb.tile([P, I], U8, name="z_scales", align_bytes=64)
         for s in range(I // Z_SLOTS):
             slots = slice(s * Z_SLOTS, (s + 1) * Z_SLOTS)
@@ -112,6 +109,8 @@ def tile_attend_latenterror_pl_kernel(tc, keys_words, keys_scales, kcopy, wd, wu
                     scales=z_scales[:, half],
                     in_=z_bf[:, half.start * PACK : half.stop * PACK],
                 )
+            if s == 1:
+                nc.vector.quantize_mx(out=wu_codes[:].bitcast(FP8X4), scales=wu_scales[:], in_=wu_bf[:])
 
         v = []
         for t in range(PACK):
@@ -126,16 +125,22 @@ def tile_attend_latenterror_pl_kernel(tc, keys_words, keys_scales, kcopy, wd, wu
                 start=True,
                 stop=True,
             )
-            v_t = sb.tile([P, I], F32, name=f"v{t}")
-            nc.scalar.copy(out=v_t[:], in_=bank[:])
-            v.append(v_t)
+            if t == 0:
+                v.append(bank)
+            else:
+                v_t = sb.tile([P, I], F32, name=f"v{t}")
+                nc.scalar.copy(out=v_t[:], in_=bank[:])
+                v.append(v_t)
 
         out_rows = out_0.rearrange("(p t) i -> p t i", t=PACK)
         y = [sb.tile([P, 2, I], F32, name=f"y{u}") for u in range(2)]
         y_bf = sb.tile([P, I, PACK], BF16, name="y_bf", align_bytes=64)
         y_codes = sb.tile([P, I], U32, name="y_codes", align_bytes=64)
         y_scales = sb.tile([P, I], U8, name="y_scales", align_bytes=64)
-        for t in range(3):
+        picked = sb.tile([P, I], F32, name="picked", tag="z_bf", align_bytes=64)
+        nc.vector.tensor_copy(out=picked[:], in_=kc[0][:].indirect(offsets[:]))
+        nc.vector.tensor_tensor(y[0][:, 0, :], picked[:], v[0][:], ADD)
+        for t in range(1, 3):
             nc.vector.tensor_tensor(y[t // 2][:, t % 2, :], kc[t][:].indirect(offsets[:]), v[t][:], ADD)
             if t == 1:
                 nc.sync.dma_start(out=out_rows[:, 0:2, :], in_=y[0][:])
@@ -155,8 +160,7 @@ def tile_attend_latenterror_pl_kernel(tc, keys_words, keys_scales, kcopy, wd, wu
             if s % 2 == 1:
                 half = slice((s - 1) * TAIL_SLOTS, (s + 1) * TAIL_SLOTS)
                 nc.sync.dma_start(out=out_rows[:, 3, half], in_=y[1][:, 1, half])
-        for h in range(2):
-            half = slice(256 * h, 256 * (h + 1))
+        for half in (slice(0, 256), slice(256, 384), slice(384, 512)):
             nc.vector.quantize_mx(
                 out=y_codes[:, half].bitcast(FP8X4),
                 scales=y_scales[:, half],

@@ -18,13 +18,12 @@ P = 128
 PACK = 4
 Z_SLOTS = 128
 TAIL_SLOTS = 128
-WD_SCALAR_COLS = 76
 
 
-def deal_weights(copy, raw, grouped, m0, m1):
+def deal_weights(copy, raw, grouped, j0, j1):
     copy(
-        out=grouped[:].rearrange("p (t m j) -> p m j t", t=PACK, j=PACK)[:, m0:m1],
-        in_=raw[:].rearrange("p j (m t) -> p m j t", t=PACK)[:, m0:m1],
+        out=grouped[:].rearrange("p (t m j) -> p m j t", t=PACK, j=PACK)[:, :, j0:j1],
+        in_=raw[:].rearrange("p j (m t) -> p m j t", t=PACK)[:, :, j0:j1],
     )
 
 
@@ -38,36 +37,46 @@ def tile_attend_latenterror_pl_kernel(tc, keys_words, keys_scales, kcopy, wd, wu
 
         pool_scales = sb.tile([P, T], U8, name="pool_scales")
         nc.vector.memset(pool_scales[:].bitcast(I32), 0)
+        key_scales = sb.tile([P, I], U8, name="key_scales", align_bytes=64)
+        nc.vector.memset(key_scales[:].bitcast(I32), 0)
 
-        wd_raw = sb.tile([P, PACK, C], F32, name="wd_raw")
-        nc.sync.dma_start(out=wd_raw[:], in_=wd.rearrange("(p j) c -> p j c", j=PACK))
-        for q in range(4):
-            nc.sync.dma_start(
-                out=pool_scales[32 * q : 32 * q + 4, :].bitcast(I32),
-                in_=keys_scales[0, 4 * q : 4 * q + 4, :].bitcast(I32),
-            )
+        wd_raw = sb.tile([P, PACK, C], F32, name="wd_raw", tag="wd_raw", align_bytes=64)
+        wd_rows = wd.rearrange("(p j) c -> p j c", j=PACK)
+        nc.sync.dma_start(out=wd_raw[:, 0:2, :], in_=wd_rows[:, 0:2, :])
         nc.sync.dma_start(offsets[:], offs)
-        pool_words = sb.tile([P, T], U32, name="pool_words")
+        nc.sync.dma_start(out=pool_scales[0:P:8, :].bitcast(I32), in_=keys_scales[0].bitcast(I32))
+        nc.sync.dma_start(out=wd_raw[:, 2:PACK, :], in_=wd_rows[:, 2:PACK, :])
+        pool_words = sb.tile([P, T], U32, name="pool_words", tag="pool_words", align_bytes=64)
         nc.sync.dma_start(
             out=pool_words[:].bitcast(I32), in_=keys_words[0].rearrange("p n t -> p (n t)").bitcast(I32)
         )
+
         wu_raw = sb.tile([P, PACK, E], F32, name="wu_raw", tag="wu_raw", align_bytes=64)
         nc.sync.dma_start(out=wu_raw[:], in_=wu.rearrange("(p j) e -> p j e", j=PACK))
+
+        wd_bf = sb.tile([P, C * PACK], BF16, name="wd_bf", tag="wd_bf", align_bytes=64)
+        deal_weights(nc.scalar.copy, wd_raw, wd_bf, 0, 2)
+        spread_scales = sb.tile([P, I], U8, name="spread_scales")
+        nc.vector.tensor_copy(out=spread_scales[:], in_=pool_scales[:].indirect(offsets[:]))
+        for r in range(4):
+            nc.scalar.dma_start(
+                out=key_scales[r:P:32, :].bitcast(I32), in_=spread_scales[8 * r : P : 32, :].bitcast(I32)
+            )
+
         kcopy_rows = kcopy.rearrange("(p t) n -> p t n", t=PACK)
         kc = []
-        for t in range(PACK):
-            plane = sb.tile([P, T], F32, name=f"kc{t}")
+
+        def load_kcopy(t, tag, align):
+            plane = sb.tile([P, T], F32, name=f"kc{t}", tag=tag, align_bytes=align)
             nc.sync.dma_start(out=plane[:], in_=kcopy_rows[:, t, :])
             kc.append(plane)
 
-        wd_bf = sb.tile([P, C * PACK], BF16, name="wd_bf", tag="w_bf", align_bytes=64)
-        deal_weights(nc.scalar.copy, wd_raw, wd_bf, 0, WD_SCALAR_COLS)
-        deal_weights(nc.vector.tensor_copy, wd_raw, wd_bf, WD_SCALAR_COLS, P)
-        key_scales = sb.tile([P, I], U8, name="key_scales", align_bytes=64)
-        nc.vector.tensor_copy(out=key_scales[:], in_=pool_scales[:].indirect(offsets[:]))
+        deal_weights(nc.vector.tensor_copy, wd_raw, wd_bf, 2, PACK)
+        load_kcopy(0, "wd_raw", 64)
         wd_codes = sb.tile([P, C], U32, name="wd_codes", align_bytes=64)
         wd_scales = sb.tile([P, C], U8, name="wd_scales", align_bytes=64)
         nc.vector.quantize_mx(out=wd_codes[:].bitcast(FP8X4), scales=wd_scales[:], in_=wd_bf[:])
+        load_kcopy(1, "wd_bf", 64)
 
         key_words = sb.tile([P, I], U32, name="key_words", align_bytes=64)
         for h in range(2):
@@ -75,9 +84,10 @@ def tile_attend_latenterror_pl_kernel(tc, keys_words, keys_scales, kcopy, wd, wu
                 out=key_words[:, 256 * h : 256 * (h + 1)],
                 in_=pool_words[:].indirect(offsets[:, 16 * h : 16 * (h + 1)]),
             )
+        load_kcopy(2, "pool_words", 64)
 
-        wu_bf = sb.tile([P, E * PACK], BF16, name="wu_bf", tag="w_bf", align_bytes=64)
-        deal_weights(nc.vector.tensor_copy, wu_raw, wu_bf, 0, P)
+        wu_bf = sb.tile([P, E * PACK], BF16, name="wu_bf", tag="wu_bf", align_bytes=64)
+        deal_weights(nc.vector.tensor_copy, wu_raw, wu_bf, 0, PACK)
         wu_codes = sb.tile([P, E], U32, name="wu_codes", align_bytes=64)
         wu_scales = sb.tile([P, E], U8, name="wu_scales", align_bytes=64)
 
@@ -111,6 +121,7 @@ def tile_attend_latenterror_pl_kernel(tc, keys_words, keys_scales, kcopy, wd, wu
                 )
             if s == 1:
                 nc.vector.quantize_mx(out=wu_codes[:].bitcast(FP8X4), scales=wu_scales[:], in_=wu_bf[:])
+                load_kcopy(3, "wu_bf", 64)
 
         v = []
         for t in range(PACK):

from contextlib import ExitStack

import concourse.mybir as mybir

D, T, I, C, E = 512, 2048, 512, 512, 512
FLOPS = 2 * D * C * I + 2 * C * E * I

F32 = mybir.dt.float32
BF16 = mybir.dt.bfloat16
I32 = mybir.dt.int32
U32 = mybir.dt.uint32
U16 = mybir.dt.uint16
U8 = mybir.dt.uint8
FP8X4 = mybir.dt.float8_e4m3fn_x4
ADD = mybir.AluOpType.add

P = 128
PACK = 4
Z_SLOTS = 128
TAIL_SLOTS = 128


def deal_weights(copy, raw, grouped, j0, j1):
    copy(
        out=grouped[:].rearrange("p (t m j) -> p m j t", t=PACK, j=PACK)[:, :, j0:j1],
        in_=raw[:].rearrange("p j (m t) -> p m j t", t=PACK)[:, :, j0:j1],
    )


def tile_attend_latenterror_pl_kernel(tc, keys_words, keys_scales, kcopy, wd, wu, offs, out_0, out_1, out_2):
    nc = tc.nc
    with ExitStack() as ctx:
        sb = ctx.enter_context(tc.tile_pool(name="sb", bufs=1))
        psum = ctx.enter_context(tc.psum_pool(name="psum", bufs=1))

        offsets = sb.tile([P, I // 16], U16, name="offsets")

        pool_scales = sb.tile([P, T], U8, name="pool_scales")
        nc.vector.memset(pool_scales[:].bitcast(I32), 0)
        key_scales = sb.tile([P, I], U8, name="key_scales", align_bytes=64)
        nc.vector.memset(key_scales[:].bitcast(I32), 0)

        wd_raw = sb.tile([P, PACK, C], F32, name="wd_raw", tag="wd_raw", align_bytes=64)
        wd_rows = wd.rearrange("(p j) c -> p j c", j=PACK)
        nc.sync.dma_start(out=wd_raw[:, 0:2, :], in_=wd_rows[:, 0:2, :])
        nc.sync.dma_start(offsets[:], offs)
        nc.sync.dma_start(out=pool_scales[0:P:8, :].bitcast(I32), in_=keys_scales[0].bitcast(I32))
        nc.sync.dma_start(out=wd_raw[:, 2:PACK, :], in_=wd_rows[:, 2:PACK, :])
        pool_words = sb.tile([P, T], U32, name="pool_words", tag="pool_words", align_bytes=64)
        nc.sync.dma_start(
            out=pool_words[:].bitcast(I32), in_=keys_words[0].rearrange("p n t -> p (n t)").bitcast(I32)
        )

        wu_raw = sb.tile([P, PACK, E], F32, name="wu_raw", tag="wu_raw", align_bytes=64)
        nc.sync.dma_start(out=wu_raw[:], in_=wu.rearrange("(p j) e -> p j e", j=PACK))

        wd_bf = sb.tile([P, C * PACK], BF16, name="wd_bf", tag="wd_bf", align_bytes=64)
        deal_weights(nc.scalar.copy, wd_raw, wd_bf, 0, 2)
        spread_scales = sb.tile([P, I], U8, name="spread_scales")
        nc.vector.tensor_copy(out=spread_scales[:], in_=pool_scales[:].indirect(offsets[:]))
        for r in range(4):
            nc.scalar.dma_start(
                out=key_scales[r:P:32, :].bitcast(I32), in_=spread_scales[8 * r : P : 32, :].bitcast(I32)
            )

        kcopy_rows = kcopy.rearrange("(p t) n -> p t n", t=PACK)
        kc = []

        def load_kcopy(t, tag, align):
            plane = sb.tile([P, T], F32, name=f"kc{t}", tag=tag, align_bytes=align)
            nc.sync.dma_start(out=plane[:], in_=kcopy_rows[:, t, :])
            kc.append(plane)

        deal_weights(nc.vector.tensor_copy, wd_raw, wd_bf, 2, PACK)
        load_kcopy(0, "wd_raw", 64)
        wd_codes = sb.tile([P, C], U32, name="wd_codes", align_bytes=64)
        wd_scales = sb.tile([P, C], U8, name="wd_scales", align_bytes=64)
        nc.vector.quantize_mx(out=wd_codes[:].bitcast(FP8X4), scales=wd_scales[:], in_=wd_bf[:])
        load_kcopy(1, "wd_bf", 64)

        key_words = sb.tile([P, I], U32, name="key_words", align_bytes=64)
        for h in range(2):
            nc.vector.tensor_copy(
                out=key_words[:, 256 * h : 256 * (h + 1)],
                in_=pool_words[:].indirect(offsets[:, 16 * h : 16 * (h + 1)]),
            )
        load_kcopy(2, "pool_words", 64)

        wu_bf = sb.tile([P, E * PACK], BF16, name="wu_bf", tag="wu_bf", align_bytes=64)
        deal_weights(nc.vector.tensor_copy, wu_raw, wu_bf, 0, PACK)
        wu_codes = sb.tile([P, E], U32, name="wu_codes", align_bytes=64)
        wu_scales = sb.tile([P, E], U8, name="wu_scales", align_bytes=64)

        z_bf = sb.tile([P, I * PACK], BF16, name="z_bf", tag="z_bf", align_bytes=64)
        z_codes = sb.tile([P, I], U32, name="z_codes", tag="wu_raw", align_bytes=64)
        z_scales = sb.tile([P, I], U8, name="z_scales", align_bytes=64)
        for s in range(I // Z_SLOTS):
            slots = slice(s * Z_SLOTS, (s + 1) * Z_SLOTS)
            bank = psum.tile([P, PACK, Z_SLOTS], F32, name=f"z_bank{s}")
            for t in range(PACK):
                cols = slice(t * P, (t + 1) * P)
                nc.tensor.matmul_mx(
                    out=bank[:, t, :],
                    lhsT=wd_codes[:, cols].bitcast(FP8X4),
                    lhsT_scale=wd_scales[:, cols],
                    rhs=key_words[:, slots].bitcast(FP8X4),
                    rhs_scale=key_scales[:, slots],
                    start=True,
                    stop=True,
                )
            nc.scalar.copy(
                out=z_bf[:, s * Z_SLOTS * PACK : (s + 1) * Z_SLOTS * PACK].rearrange("p (n t) -> p n t", t=PACK),
                in_=bank[:].rearrange("p t n -> p n t"),
            )
            if s % 2 == 1:
                half = slice((s - 1) * Z_SLOTS, (s + 1) * Z_SLOTS)
                nc.vector.quantize_mx(
                    out=z_codes[:, half].bitcast(FP8X4),
                    scales=z_scales[:, half],
                    in_=z_bf[:, half.start * PACK : half.stop * PACK],
                )
            if s == 1:
                nc.vector.quantize_mx(out=wu_codes[:].bitcast(FP8X4), scales=wu_scales[:], in_=wu_bf[:])
                load_kcopy(3, "wu_bf", 64)

        v = []
        for t in range(PACK):
            cols = slice(t * P, (t + 1) * P)
            bank = psum.tile([P, I], F32, name=f"v_bank{t}")
            nc.tensor.matmul_mx(
                out=bank[:],
                lhsT=wu_codes[:, cols].bitcast(FP8X4),
                lhsT_scale=wu_scales[:, cols],
                rhs=z_codes[:].bitcast(FP8X4),
                rhs_scale=z_scales[:],
                start=True,
                stop=True,
            )
            if t == 0:
                v.append(bank)
            else:
                v_t = sb.tile([P, I], F32, name=f"v{t}")
                nc.scalar.copy(out=v_t[:], in_=bank[:])
                v.append(v_t)

        out_rows = out_0.rearrange("(p t) i -> p t i", t=PACK)
        y = [sb.tile([P, 2, I], F32, name=f"y{u}") for u in range(2)]
        y_bf = sb.tile([P, I, PACK], BF16, name="y_bf", align_bytes=64)
        y_codes = sb.tile([P, I], U32, name="y_codes", align_bytes=64)
        y_scales = sb.tile([P, I], U8, name="y_scales", align_bytes=64)
        picked = sb.tile([P, I], F32, name="picked", tag="z_bf", align_bytes=64)
        nc.vector.tensor_copy(out=picked[:], in_=kc[0][:].indirect(offsets[:]))
        nc.vector.tensor_tensor(y[0][:, 0, :], picked[:], v[0][:], ADD)
        for t in range(1, 3):
            nc.vector.tensor_tensor(y[t // 2][:, t % 2, :], kc[t][:].indirect(offsets[:]), v[t][:], ADD)
            if t == 1:
                nc.sync.dma_start(out=out_rows[:, 0:2, :], in_=y[0][:])
                nc.scalar.copy(out=y_bf[:, :, 0:2], in_=y[0][:].rearrange("p t i -> p i t"))
        nc.sync.dma_start(out=out_rows[:, 2, :], in_=y[1][:, 0, :])
        words_out = out_1[0].rearrange("p i t -> p (i t)").bitcast(I32)
        n_tail = I // TAIL_SLOTS
        for s in range(n_tail):
            slots = slice(s * TAIL_SLOTS, (s + 1) * TAIL_SLOTS)
            nc.vector.tensor_tensor(
                y[1][:, 1, slots],
                kc[3][:].indirect(offsets[:, slots.start // 16 : slots.stop // 16]),
                v[3][:, slots],
                ADD,
            )
            nc.scalar.copy(out=y_bf[:, slots, 2:4], in_=y[1][:, :, slots].rearrange("p t i -> p i t"))
            if s % 2 == 1:
                half = slice((s - 1) * TAIL_SLOTS, (s + 1) * TAIL_SLOTS)
                nc.sync.dma_start(out=out_rows[:, 3, half], in_=y[1][:, 1, half])
        for half in (slice(0, 256), slice(256, 384), slice(384, 512)):
            nc.vector.quantize_mx(
                out=y_codes[:, half].bitcast(FP8X4),
                scales=y_scales[:, half],
                in_=y_bf[:, half, :].rearrange("p i t -> p (i t)"),
            )
            nc.sync.dma_start(out=words_out[:, half], in_=y_codes[:, half].bitcast(I32))
        for q in range(4):
            eng = nc.scalar if q % 2 == 0 else nc.sync
            eng.dma_start(
                out=out_2[0, 4 * q : 4 * q + 4, :].bitcast(I32),
                in_=y_scales[32 * q : 32 * q + 4, :].bitcast(I32),
            )
